import numpy as np
import ml_dtypes


def mxq(x, axis, fmt="e4m3"):
    dtype, down = {"e4m3": (ml_dtypes.float8_e4m3fn, 7), "e5m2": (ml_dtypes.float8_e5m2, 14)}[fmt]
    v = np.moveaxis(np.asarray(x, np.float32).astype(ml_dtypes.bfloat16).astype(np.float64), axis, -1)
    blocks = v.reshape(v.shape[:-1] + (-1, 32))
    amax = np.abs(blocks).max(-1, keepdims=True)
    byte = np.maximum(np.where(amax > 0, np.frexp(amax)[1] - 1 + 127, 0) - down, 1)
    scale = np.exp2(byte - 127.0)
    codes = (blocks / scale).astype(np.float32).astype(dtype).astype(np.float64)
    return np.moveaxis((codes * scale).reshape(v.shape), -1, axis)


WIDE = False


def mx_kscale(k):
    if not WIDE:
        return np.ones(k)
    levels = np.array([10, -10, 5, -5, 0])
    if k % 512:
        return np.exp2(np.random.permutation(np.resize(levels, k // 32))).repeat(32)
    a = np.empty((k // 512, 16))
    for p in range(k // 512):
        a[p, :8] = np.random.permutation(np.resize(levels, 8))
        for g in range(8):
            far = levels[np.abs(levels - a[p, g]) >= 10]
            a[p, g + 8] = far[np.random.randint(len(far))]
    return np.exp2(a.ravel()).repeat(32)


def f64(x):
    return np.asarray(x).astype(np.float64)


def striped(idx):
    return np.tile(idx.reshape(-1, 16).T, (8, 1)).astype(np.uint16)


def unstriped(offs):
    return offs[:16].T.reshape(-1).astype(np.int64)


K, T, E, C, N = 256, 512, 6, 256, 512
TOP = 3


def by_expert(wq, xq):
    return np.concatenate([wq[e].T @ xq[:, e * C:(e + 1) * C] for e in range(E)], axis=1)


def setup_inputs():
    n = np.random.standard_normal
    s = mx_kscale(N)[:, None]
    deal = np.repeat(np.arange(E), C).reshape(TOP, T)[:, np.random.permutation(T)]
    deal = np.take_along_axis(deal, np.argsort(np.random.rand(TOP, T), axis=0), axis=0)
    for _ in range(8):
        s_, t_ = np.random.permutation(T).reshape(2, -1); r = np.random.randint(TOP, size=T // 2); x, y = deal[r, s_].copy(), deal[r, t_].copy()
        ok = ~((deal[:, s_] == y).any(0) | (deal[:, t_] == x).any(0)); deal[r[ok], s_[ok]] = y[ok]; deal[r[ok], t_[ok]] = x[ok]
    order = np.lexsort((np.random.rand(TOP * T), deal.reshape(-1)))
    slot_token = order % T; pos = np.empty(TOP * T, np.int64); pos[order] = np.arange(TOP * T); pos = pos.reshape(TOP, T)
    g = np.random.uniform(0.5, 1.5, (TOP, T)); g = g / g.sum(0)
    w_slot = np.empty(E * C)
    for r in range(TOP): w_slot[pos[r]] = g[r]
    return {
        "dyT": (n((N, T)) * s).astype(np.float32),
        "w": (n((E + 1, N, K)) / np.sqrt(N) / s[None]).astype(np.float32),
        "gate": np.tile(w_slot, (N, 1)).astype(np.float32),
        "offs": striped(slot_token),
        "pos1": striped(pos[0]),
        "pos2": striped(pos[1]),
        "pos3": striped(pos[2]),
    }


def reference(dyT, w, gate, offs, pos1, pos2, pos3):
    idx = unstriped(offs)
    gq = mxq(f64(gate) * f64(dyT)[:, idx], 0, "e4m3")
    wq = mxq(f64(w), 1, "e4m3")
    ds = wq[E].T @ mxq(f64(dyT), 0, "e4m3")
    dx = by_expert(wq, gq)
    return ds + dx[:, unstriped(pos1)] + dx[:, unstriped(pos2)] + dx[:, unstriped(pos3)]

@@ -1,0 +1,197 @@
+from contextlib import ExitStack
+
+import concourse.mybir as mybir
+
+K, T, E, C, N = 256, 512, 6, 256, 512
+S = E * C
+P = 128
+PACK = 4
+RUN = 4
+HALF = T // 2
+
+FLOPS = 2 * N * K * (S + T)
+BYTES = 4 * (N * T + (E + 1) * N * K + S + K * T) + 2 * P * (S + 3 * T) // 16
+
+F32 = mybir.dt.float32
+BF16 = mybir.dt.bfloat16
+U32 = mybir.dt.uint32
+U16 = mybir.dt.uint16
+U8 = mybir.dt.uint8
+FP8X4 = mybir.dt.float8_e4m3fn_x4
+MULT = mybir.AluOpType.mult
+ADD = mybir.AluOpType.add
+
+
+def tile_moe_bds_lin_none_kernel(tc, dyT, w, gate, offs, pos1, pos2, pos3, out):
+    nc = tc.nc
+    with ExitStack() as ctx:
+        keep = ctx.enter_context(tc.tile_pool(name="keep", bufs=1))
+        psum = ctx.enter_context(tc.psum_pool(name="psum", bufs=8))
+
+        def load(name, shape, dtype, src):
+            tl = keep.tile(shape, dtype, name=name, tag=name, align_bytes=64)
+            nc.sync.dma_start(tl[:], src)
+            return tl
+
+        dy_rows = dyT.rearrange("(p j) c -> p j c", j=PACK)
+
+        def load_w(e):
+            return load("w%d" % e, [P, PACK, K], F32, w[e].rearrange("(p j) k -> p j k", j=PACK))
+
+        def load_gate(c0, c1):
+            return load("gate%d" % c0, [P, (c1 - c0) * C], F32, gate[0:P, c0 * C : c1 * C])
+
+        slots = load("slots", [P, S // 16], U16, offs)
+        dy = [load("dy0", [P, T], F32, dy_rows[:, 0, :])]
+        g0 = load_gate(0, 1)
+        for j in range(1, PACK):
+            dy.append(load("dy%d" % j, [P, T], F32, dy_rows[:, j, :]))
+        g1 = load_gate(1, 2)
+        w_raw = [load_w(0)]
+        g2 = load_gate(2, 4)
+        w_raw.append(load_w(1))
+        g4 = load_gate(4, 6)
+        for e in range(2, E + 1):
+            w_raw.append(load_w(e))
+        back = [load("back%d" % r, [P, T // 16], U16, lst) for r, lst in enumerate((pos1, pos2, pos3))]
+        gates = [g0[:], g1[:], g2[:, 0:C], g2[:, C : 2 * C], g4[:, 0:C], g4[:, C : 2 * C]]
+
+        def weave(copy, woven, planes):
+            copy(
+                woven.rearrange("p (c i t) -> p c t i", i=RUN, t=PACK),
+                planes.rearrange("p t (c i) -> p c t i", i=RUN),
+            )
+
+        def fresh(name, shape, dtype, tag=None):
+            return keep.tile(shape, dtype, name=name, tag=tag or name, align_bytes=64)
+
+        def quantize(codes, scales, woven):
+            nc.vector.quantize_mx(out=codes.bitcast(FP8X4), scales=scales, in_=woven)
+            return codes, scales
+
+        def quantize_fresh(name, woven, width, tag=None):
+            codes = fresh(name + "_codes", [P, width], U32, tag)
+            scales = fresh(name + "_scales", [P, width], U8)
+            return quantize(codes[:], scales[:], woven[:])
+
+        def product(acc, wq, xq):
+            nc.tensor.matmul_mx(
+                out=acc, lhsT=wq[0].bitcast(FP8X4), lhsT_scale=wq[1],
+                rhs=xq[0].bitcast(FP8X4), rhs_scale=xq[1], start=True, stop=True,
+            )
+
+        dx = [keep.tile([P, S], F32, name="dx%d" % m) for m in range(2)]
+        ds = [keep.tile([P, T], F32, name="ds%d" % m) for m in range(2)]
+        upper = fresh("upper", [P, (E + 1) * P * PACK], BF16)
+        planes, gb, gq, lower, wq = {}, {}, {}, {}, {}
+        after_w = {1: "w0", 2: "w2", 3: "w3", 4: "w4", 5: "w5"}
+
+        def gather(e):
+            planes[e] = fresh("planes%d" % e, [P, PACK, C], F32, after_w.get(e - 2, "gb0") if e >= 2 else None)
+            lst = slots[:, e * C // 16 : (e + 1) * C // 16]
+            for j in range(PACK):
+                nc.vector.tensor_tensor(planes[e][:, j, :], dy[j][:].indirect(lst), gates[e], MULT)
+
+        def weave_g(e):
+            gb[e] = fresh("gb%d" % e, [P, C * PACK], BF16, after_w.get(e))
+            weave(nc.scalar.copy, gb[e][:], planes[e][:])
+
+        def weave_lower(e):
+            lower[e] = fresh("lower%d" % e, [P, P * PACK], BF16)
+            weave(nc.scalar.copy, lower[e][:], w_raw[e][:, :, 0:P])
+
+        def weave_upper(e):
+            weave(nc.scalar.copy, upper[:, e * P * PACK : (e + 1) * P * PACK], w_raw[e][:, :, P:K])
+
+        def quantize_g(e):
+            gq[e] = quantize_fresh("g%d" % e, gb[e], C)
+
+        def quantize_lower(e):
+            wq[(e, 0)] = quantize_fresh("lower%d" % e, lower[e], P)
+
+        def experts(m, es):
+            acc = psum.tile([P, T], F32, name="acc")
+            for i, e in enumerate(es):
+                product(acc[:, i * C : (i + 1) * C], wq[(e, m)], gq[e])
+            nc.scalar.copy(dx[m][:, es[0] * C : (es[-1] + 1) * C], acc[:, 0 : len(es) * C])
+
+        def shared(m, dyq):
+            acc = psum.tile([P, T], F32, name="acc")
+            product(acc[:], wq[(E, m)], dyq)
+            nc.scalar.copy(ds[m][:], acc[:])
+
+        def combine(m):
+            part = [[ds[m][:, h * HALF : (h + 1) * HALF] for h in range(2)]]
+            for r in range(3):
+                nxt = []
+                for h in range(2):
+                    tl = keep.tile([P, HALF], F32, name="sum%d_%d_%d" % (m, r, h))
+                    lst = back[r][:, h * HALF // 16 : (h + 1) * HALF // 16]
+                    nc.vector.tensor_tensor(tl[:], dx[m][:].indirect(lst), part[r][h], ADD)
+                    nxt.append(tl[:])
+                    if r == 2:
+                        nc.sync.dma_start(out[m * P : (m + 1) * P, h * HALF : (h + 1) * HALF], tl[:])
+                part.append(nxt)
+
+        dyb = keep.tile([P, PACK, T], BF16, name="dyb")
+        for j in range(PACK):
+            nc.scalar.copy(dyb[:, j, :], dy[j][:])
+
+        gather(0)
+        gather(1)
+        weave_g(0)
+        weave_lower(0)
+        weave_upper(0)
+        weave_lower(1)
+        quantize_g(0)
+        quantize_lower(0)
+        gather(2)
+        weave_g(1)
+        weave_upper(1)
+        weave_lower(2)
+        weave_upper(2)
+        quantize_lower(1)
+        quantize_g(1)
+        gather(3)
+        weave_g(2)
+        experts(0, [0, 1])
+        weave_lower(3)
+        weave_upper(3)
+        quantize_lower(2)
+        quantize_g(2)
+        gather(4)
+        weave_g(3)
+        weave_lower(4)
+        weave_upper(4)
+        weave_lower(5)
+        quantize_lower(3)
+        dyw = fresh("dyw", [P, T * PACK], BF16, "lower3")
+        weave(nc.vector.tensor_copy, dyw[:], dyb[:])
+        quantize_g(3)
+        quantize_lower(4)
+        gather(5)
+        weave_g(4)
+        weave_upper(5)
+        weave_lower(6)
+        experts(0, [2, 3])
+        weave_upper(6)
+        weave_g(5)
+        quantize_g(4)
+        dyq = quantize_fresh("dy", dyw, T, "gate4")
+        quantize_lower(6)
+        quantize_lower(5)
+        quantize_g(5)
+        experts(0, [4])
+        shared(0, dyq)
+        experts(0, [5])
+        up_codes = fresh("up_codes", [P, (E + 1) * P], U32, "w5")
+        up_scales = fresh("up_scales", [P, (E + 1) * P], U8)
+        for e0, e1 in ((0, 4), (4, 6), (6, 7)):
+            quantize(up_codes[:, e0 * P : e1 * P], up_scales[:, e0 * P : e1 * P], upper[:, e0 * P * PACK : e1 * P * PACK])
+        for e in range(E + 1):
+            wq[(e, 1)] = (up_codes[:, e * P : (e + 1) * P], up_scales[:, e * P : (e + 1) * P])
+        for e in range(0, E, 2):
+            experts(1, [e, e + 1])
+        shared(1, dyq)
+        combine(0)
+        combine(1)

@@ -35,8 +35,11 @@ def tile_moe_bds_lin_none_kernel(tc, dyT, w, gate, offs, pos1, pos2, pos3, out):
 
         dy_rows = dyT.rearrange("(p j) c -> p j c", j=PACK)
 
-        def load_w(e):
-            return load("w%d" % e, [P, PACK, K], F32, w[e].rearrange("(p j) k -> p j k", j=PACK))
+        def load_w(name, es):
+            tl = keep.tile([P, len(es), PACK, K], F32, name=name, tag=name, align_bytes=64)
+            for i, e in enumerate(es):
+                nc.sync.dma_start(tl[:, i], w[e].rearrange("(p j) k -> p j k", j=PACK))
+            return tl
 
         def load_gate(c0, c1):
             return load("gate%d" % c0, [P, (c1 - c0) * C], F32, gate[0:P, c0 * C : c1 * C])
@@ -44,17 +47,19 @@ def tile_moe_bds_lin_none_kernel(tc, dyT, w, gate, offs, pos1, pos2, pos3, out):
         slots = load("slots", [P, S // 16], U16, offs)
         dy = [load("dy0", [P, T], F32, dy_rows[:, 0, :])]
         g0 = load_gate(0, 1)
-        for j in range(1, PACK):
-            dy.append(load("dy%d" % j, [P, T], F32, dy_rows[:, j, :]))
         g1 = load_gate(1, 2)
-        w_raw = [load_w(0)]
+        for j in (1, 2):
+            dy.append(load("dy%d" % j, [P, T], F32, dy_rows[:, j, :]))
+        w0 = load_w("w0", [0])
+        dy.append(load("dy3", [P, T], F32, dy_rows[:, 3, :]))
         g2 = load_gate(2, 4)
-        w_raw.append(load_w(1))
+        w1 = load_w("w1", [1])
         g4 = load_gate(4, 6)
-        for e in range(2, E + 1):
-            w_raw.append(load_w(e))
+        w23 = load_w("w23", [2, 3])
+        w465 = load_w("w465", [4, 6, 5])
         back = [load("back%d" % r, [P, T // 16], U16, lst) for r, lst in enumerate((pos1, pos2, pos3))]
-        gates = [g0[:], g1[:], g2[:, 0:C], g2[:, C : 2 * C], g4[:, 0:C], g4[:, C : 2 * C]]
+        gates = [g0[:], g1[:], g2[:, 0:C], g2[:, C : 2 * C], g4[:, 0:C], g4[:, C : C + P], g4[:, C + P : 2 * C]]
+        first = [0, C, 2 * C, 3 * C, 4 * C, 5 * C, 5 * C + P, S]
 
         def weave(copy, woven, planes):
             copy(
@@ -72,7 +77,7 @@ def tile_moe_bds_lin_none_kernel(tc, dyT, w, gate, offs, pos1, pos2, pos3, out):
         def quantize_fresh(name, woven, width, tag=None):
             codes = fresh(name + "_codes", [P, width], U32, tag)
             scales = fresh(name + "_scales", [P, width], U8)
-            return quantize(codes[:], scales[:], woven[:])
+            return quantize(codes[:], scales[:], woven[:, :])
 
         def product(acc, wq, xq):
             nc.tensor.matmul_mx(
@@ -81,117 +86,131 @@ def tile_moe_bds_lin_none_kernel(tc, dyT, w, gate, offs, pos1, pos2, pos3, out):
             )
 
         dx = [keep.tile([P, S], F32, name="dx%d" % m) for m in range(2)]
-        ds = [keep.tile([P, T], F32, name="ds%d" % m) for m in range(2)]
-        upper = fresh("upper", [P, (E + 1) * P * PACK], BF16)
-        planes, gb, gq, lower, wq = {}, {}, {}, {}, {}
-        after_w = {1: "w0", 2: "w2", 3: "w3", 4: "w4", 5: "w5"}
+        cuts = [(0, HALF, T), (0, T - P, T)]
+        planes, gb, gq, wq, ds = {}, {}, {}, {}, {}
 
-        def gather(e):
-            planes[e] = fresh("planes%d" % e, [P, PACK, C], F32, after_w.get(e - 2, "gb0") if e >= 2 else None)
-            lst = slots[:, e * C // 16 : (e + 1) * C // 16]
+        def gather_plane(dst, c, j):
+            lst = slots[:, first[c] // 16 : first[c + 1] // 16]
+            nc.vector.tensor_tensor(dst, dy[j][:].indirect(lst), gates[c], MULT)
+
+        def gather(c, tag=None):
+            planes[c] = fresh("planes%d" % c, [P, PACK, first[c + 1] - first[c]], F32, tag)
             for j in range(PACK):
-                nc.vector.tensor_tensor(planes[e][:, j, :], dy[j][:].indirect(lst), gates[e], MULT)
+                gather_plane(planes[c][:, j, :], c, j)
 
-        def weave_g(e):
-            gb[e] = fresh("gb%d" % e, [P, C * PACK], BF16, after_w.get(e))
-            weave(nc.scalar.copy, gb[e][:], planes[e][:])
+        def weave_g(c, width):
+            gb[c] = fresh("gb%d" % c, [P, width * PACK], BF16)
+            weave(nc.scalar.copy, gb[c][:], planes[c][:])
 
-        def weave_lower(e):
-            lower[e] = fresh("lower%d" % e, [P, P * PACK], BF16)
-            weave(nc.scalar.copy, lower[e][:], w_raw[e][:, :, 0:P])
+        def weave_w(name, raw, k0, k1, tag=None, copy=nc.scalar.copy):
+            n = raw.shape[1]
+            woven = fresh(name, [P, n * (k1 - k0) * PACK], BF16, tag)
+            copy(
+                woven[:].rearrange("p (e c i t) -> p e c t i", e=n, i=RUN, t=PACK),
+                raw[:, :, :, k0:k1].rearrange("p e t (c i) -> p e c t i", i=RUN),
+            )
+            return woven
 
-        def weave_upper(e):
-            weave(nc.scalar.copy, upper[:, e * P * PACK : (e + 1) * P * PACK], w_raw[e][:, :, P:K])
+        def columns(q, c0, c1):
+            return q[0][:, c0:c1], q[1][:, c0:c1]
 
-        def quantize_g(e):
-            gq[e] = quantize_fresh("g%d" % e, gb[e], C)
+        def quantize_g(c):
+            gq[c] = quantize_fresh("g%d" % c, gb[c], first[c + 1] - first[c])
 
-        def quantize_lower(e):
-            wq[(e, 0)] = quantize_fresh("lower%d" % e, lower[e], P)
-
-        def experts(m, es):
-            acc = psum.tile([P, T], F32, name="acc")
+        def quantize_w(name, woven, es, m):
+            q = quantize_fresh(name, woven, len(es) * P)
             for i, e in enumerate(es):
-                product(acc[:, i * C : (i + 1) * C], wq[(e, m)], gq[e])
-            nc.scalar.copy(dx[m][:, es[0] * C : (es[-1] + 1) * C], acc[:, 0 : len(es) * C])
+                wq[(e, m)] = columns(q, i * P, (i + 1) * P)
 
-        def shared(m, dyq):
+        def experts(m, cs):
             acc = psum.tile([P, T], F32, name="acc")
-            product(acc[:], wq[(E, m)], dyq)
-            nc.scalar.copy(ds[m][:], acc[:])
+            s0, s1 = first[cs[0]], first[cs[-1] + 1]
+            for c in cs:
+                product(acc[:, first[c] - s0 : first[c + 1] - s0], wq[(first[c] // C, m)], gq[c])
+            nc.scalar.copy(dx[m][:, s0:s1], acc[:, 0 : s1 - s0])
 
-        def combine(m):
-            part = [[ds[m][:, h * HALF : (h + 1) * HALF] for h in range(2)]]
-            for r in range(3):
-                nxt = []
+        def shared(name, m, dyq, c0, c1):
+            acc = psum.tile([P, T], F32, name="acc")
+            product(acc[:, 0 : c1 - c0], wq[(E, m)], columns(dyq, c0, c1))
+            tl = fresh(name, [P, c1 - c0], F32)
+            nc.scalar.copy(tl[:], acc[:, 0 : c1 - c0])
+            return tl
+
+        def combine(m, part, rounds):
+            for r in rounds:
                 for h in range(2):
-                    tl = keep.tile([P, HALF], F32, name="sum%d_%d_%d" % (m, r, h))
-                    lst = back[r][:, h * HALF // 16 : (h + 1) * HALF // 16]
-                    nc.vector.tensor_tensor(tl[:], dx[m][:].indirect(lst), part[r][h], ADD)
-                    nxt.append(tl[:])
+                    c0, c1 = cuts[m][h], cuts[m][h + 1]
+                    tl = fresh("sum%d_%d_%d" % (m, r, h), [P, c1 - c0], F32, None)
+                    nc.vector.tensor_tensor(tl[:], dx[m][:].indirect(back[r][:, c0 // 16 : c1 // 16]), part[h], ADD)
+                    part[h] = tl[:]
                     if r == 2:
-                        nc.sync.dma_start(out[m * P : (m + 1) * P, h * HALF : (h + 1) * HALF], tl[:])
-                part.append(nxt)
+                        nc.sync.dma_start(out[m * P : (m + 1) * P, c0:c1], tl[:])
 
-        dyb = keep.tile([P, PACK, T], BF16, name="dyb")
+        pairs = fresh("pairs", [P, 2, 2 * T], BF16)
+
+        def cast_plane(j):
+            nc.scalar.copy(pairs[:, j // 2, j % 2 : 2 * T : 2], dy[j][:])
+
+        planes[0] = fresh("planes0", [P, PACK, 2 * C], F32)
         for j in range(PACK):
-            nc.scalar.copy(dyb[:, j, :], dy[j][:])
-
-        gather(0)
-        gather(1)
-        weave_g(0)
-        weave_lower(0)
-        weave_upper(0)
-        weave_lower(1)
-        quantize_g(0)
-        quantize_lower(0)
+            gather_plane(planes[0][:, j, 0:C], 0, j)
+            gather_plane(planes[0][:, j, C : 2 * C], 1, j)
+        for j in range(3):
+            cast_plane(j)
+        both0 = weave_w("both0", w0[:], 0, K)
+        cast_plane(3)
+        quantize_w("lower0", both0[:, 0 : P * PACK], [0], 0)
         gather(2)
-        weave_g(1)
-        weave_upper(1)
-        weave_lower(2)
-        weave_upper(2)
-        quantize_lower(1)
-        quantize_g(1)
-        gather(3)
-        weave_g(2)
-        experts(0, [0, 1])
-        weave_lower(3)
-        weave_upper(3)
-        quantize_lower(2)
+        weave_g(0, 2 * C)
+        g01 = quantize_fresh("g01", gb[0], 2 * C)
+        gq[0], gq[1] = columns(g01, 0, C), columns(g01, C, 2 * C)
+        gather(3, "gb0")
+        both1 = weave_w("both1", w1[:], 0, K)
+        weave_g(2, C)
+        quantize_w("lower1", both1[:, 0 : P * PACK], [1], 0)
         quantize_g(2)
-        gather(4)
-        weave_g(3)
-        weave_lower(4)
-        weave_upper(4)
-        weave_lower(5)
-        quantize_lower(3)
-        dyw = fresh("dyw", [P, T * PACK], BF16, "lower3")
-        weave(nc.vector.tensor_copy, dyw[:], dyb[:])
+        gather(4, "gb2")
+        lower23 = weave_w("lower23", w23[:], 0, P)
+        weave_g(3, C)
+        experts(0, [0, 1])
+        quantize_w("lower23", lower23, [2, 3], 0)
+        dyw = fresh("dyw", [P, T * PACK], BF16, "lower23")
+        nc.vector.tensor_copy(
+            dyw[:].bitcast(F32).rearrange("p (c i u) -> p c u i", i=RUN, u=2),
+            pairs[:].bitcast(F32).rearrange("p u (c i) -> p c u i", i=RUN),
+        )
         quantize_g(3)
-        quantize_lower(4)
-        gather(5)
-        weave_g(4)
-        weave_upper(5)
-        weave_lower(6)
+        gather(5, "gb3")
+        lower46 = weave_w("lower46", w465[:, 0:2], 0, P)
+        weave_g(4, C)
         experts(0, [2, 3])
-        weave_upper(6)
-        weave_g(5)
+        quantize_w("lower46", lower46, [4, 6], 0)
         quantize_g(4)
-        dyq = quantize_fresh("dy", dyw, T, "gate4")
-        quantize_lower(6)
-        quantize_lower(5)
-        quantize_g(5)
+        gather(6, "gb4")
+        lower5 = weave_w("lower5", w465[:, 2:3], 0, P)
+        weave_g(5, P)
+        upper23 = weave_w("upper23", w23[:], P, K)
+        weave_g(6, P)
+        upper4 = weave_w("upper4", w465[:, 0:1], P, K)
         experts(0, [4])
-        shared(0, dyq)
-        experts(0, [5])
-        up_codes = fresh("up_codes", [P, (E + 1) * P], U32, "w5")
-        up_scales = fresh("up_scales", [P, (E + 1) * P], U8)
-        for e0, e1 in ((0, 4), (4, 6), (6, 7)):
-            quantize(up_codes[:, e0 * P : e1 * P], up_scales[:, e0 * P : e1 * P], upper[:, e0 * P * PACK : e1 * P * PACK])
-        for e in range(E + 1):
-            wq[(e, 1)] = (up_codes[:, e * P : (e + 1) * P], up_scales[:, e * P : (e + 1) * P])
-        for e in range(0, E, 2):
-            experts(1, [e, e + 1])
-        shared(1, dyq)
-        combine(0)
-        combine(1)
+        dyq = quantize_fresh("dy", dyw, T, "gate4")
+        quantize_w("lower5", lower5, [5], 0)
+        quantize_g(5)
+        quantize_g(6)
+        ds0a = shared("ds0a", 0, dyq, 0, HALF)
+        experts(0, [5, 6])
+        ds0b = shared("ds0b", 0, dyq, HALF, T)
+        upper65 = weave_w("upper65", w465[:, 1:3], P, K, "gb4", nc.vector.tensor_copy)
+        up = (fresh("up_codes", [P, (E + 1) * P], U32, "gb6")[:], fresh("up_scales", [P, (E + 1) * P], U8)[:])
+        quantize(*columns(up, 0, P), both0[:, P * PACK : K * PACK])
+        quantize(*columns(up, P, 2 * P), both1[:, P * PACK : K * PACK])
+        quantize(*columns(up, 2 * P, 4 * P), upper23[:])
+        quantize(*columns(up, 4 * P, 5 * P), upper4[:])
+        quantize(*columns(up, 5 * P, 7 * P), upper65[:])
+        for i, e in enumerate((0, 1, 2, 3, 4, 6, 5)):
+            wq[(e, 1)] = columns(up, i * P, (i + 1) * P)
+        for cs in ([0, 1], [2, 3], [4, 5, 6]):
+            experts(1, cs)
+        ds1 = shared("ds1", 1, dyq, 0, T)
+        combine(0, [ds0a[:], ds0b[:]], [0, 1, 2])
+        combine(1, [ds1[:, 0 : T - P], ds1[:, T - P : T]], [0, 1, 2])

@@ -8,6 +8,7 @@ P = 128
 PACK = 4
 RUN = 4
 HALF = T // 2
+SPARE = 16
 
 FLOPS = 2 * N * K * (S + T)
 BYTES = 4 * (N * T + (E + 1) * N * K + S + K * T) + 2 * P * (S + 3 * T) // 16
@@ -44,21 +45,29 @@ def tile_moe_bds_lin_none_kernel(tc, dyT, w, gate, offs, pos1, pos2, pos3, out):
         def load_gate(c0, c1):
             return load("gate%d" % c0, [P, (c1 - c0) * C], F32, gate[0:P, c0 * C : c1 * C])
 
+        def load_plane(j):
+            tl = keep.tile([P, T + SPARE], F32, name="dy%d" % j)
+            nc.gpsimd.memset(tl[:, T : T + SPARE], 0.0)
+            nc.sync.dma_start(tl[:, 0:T], dy_rows[:, j, :])
+            return tl
+
+        dy = [load_plane(0)]
         slots = load("slots", [P, S // 16], U16, offs)
-        dy = [load("dy0", [P, T], F32, dy_rows[:, 0, :])]
-        g0 = load_gate(0, 1)
-        g1 = load_gate(1, 2)
-        for j in (1, 2):
-            dy.append(load("dy%d" % j, [P, T], F32, dy_rows[:, j, :]))
+        g01 = keep.tile([P, 2 * C], F32, name="gate01")
+        for e in range(2):
+            nc.sync.dma_start(g01[:, e * C : (e + 1) * C], gate[0:P, e * C : (e + 1) * C])
+        dy.extend(load_plane(j) for j in (1, 2))
         w0 = load_w("w0", [0])
-        dy.append(load("dy3", [P, T], F32, dy_rows[:, 3, :]))
+        dy.append(load_plane(3))
         g2 = load_gate(2, 4)
         w1 = load_w("w1", [1])
+        w2 = load_w("w2", [2])
+        w3 = load_w("w3", [3])
         g4 = load_gate(4, 6)
-        w23 = load_w("w23", [2, 3])
-        w465 = load_w("w465", [4, 6, 5])
+        w56 = load_w("w56", [5, 6])
+        w4 = load_w("w4", [4])
         back = [load("back%d" % r, [P, T // 16], U16, lst) for r, lst in enumerate((pos1, pos2, pos3))]
-        gates = [g0[:], g1[:], g2[:, 0:C], g2[:, C : 2 * C], g4[:, 0:C], g4[:, C : C + P], g4[:, C + P : 2 * C]]
+        gates = [g01, g2, g4]
         first = [0, C, 2 * C, 3 * C, 4 * C, 5 * C, 5 * C + P, S]
 
         def weave(copy, woven, planes):
@@ -89,23 +98,23 @@ def tile_moe_bds_lin_none_kernel(tc, dyT, w, gate, offs, pos1, pos2, pos3, out):
         cuts = [(0, HALF, T), (0, T - P, T)]
         planes, gb, gq, wq, ds = {}, {}, {}, {}, {}
 
-        def gather_plane(dst, c, j):
-            lst = slots[:, first[c] // 16 : first[c + 1] // 16]
-            nc.vector.tensor_tensor(dst, dy[j][:].indirect(lst), gates[c], MULT)
+        def gather_plane(dst, j, s0, s1):
+            g, o = divmod(s0, 2 * C)
+            nc.vector.tensor_tensor(dst, dy[j][:].indirect(slots[:, s0 // 16 : s1 // 16]), gates[g][:, o : o + s1 - s0], MULT)
 
-        def gather(c, tag=None):
-            planes[c] = fresh("planes%d" % c, [P, PACK, first[c + 1] - first[c]], F32, tag)
+        def gather(c, c1, tag=None):
+            planes[c] = fresh("planes%d" % c, [P, PACK, first[c1] - first[c]], F32, tag)
             for j in range(PACK):
-                gather_plane(planes[c][:, j, :], c, j)
+                gather_plane(planes[c][:, j, :], j, first[c], first[c1])
 
-        def weave_g(c, width):
-            gb[c] = fresh("gb%d" % c, [P, width * PACK], BF16)
+        def weave_g(c, width, tag=None):
+            gb[c] = fresh("gb%d" % c, [P, width * PACK], BF16, tag)
             weave(nc.scalar.copy, gb[c][:], planes[c][:])
 
-        def weave_w(name, raw, k0, k1, tag=None, copy=nc.scalar.copy):
+        def weave_w(name, raw, k0, k1):
             n = raw.shape[1]
-            woven = fresh(name, [P, n * (k1 - k0) * PACK], BF16, tag)
-            copy(
+            woven = fresh(name, [P, n * (k1 - k0) * PACK], BF16)
+            nc.scalar.copy(
                 woven[:].rearrange("p (e c i t) -> p e c t i", e=n, i=RUN, t=PACK),
                 raw[:, :, :, k0:k1].rearrange("p e t (c i) -> p e c t i", i=RUN),
             )
@@ -149,66 +158,65 @@ def tile_moe_bds_lin_none_kernel(tc, dyT, w, gate, offs, pos1, pos2, pos3, out):
         pairs = fresh("pairs", [P, 2, 2 * T], BF16)
 
         def cast_plane(j):
-            nc.scalar.copy(pairs[:, j // 2, j % 2 : 2 * T : 2], dy[j][:])
+            nc.scalar.copy(pairs[:, j // 2, j % 2 : 2 * T : 2], dy[j][:, 0:T])
+
+        def quantize_pair(c):
+            q = quantize_fresh("g%d" % c, gb[c], 2 * C)
+            gq[c], gq[c + 1] = columns(q, 0, C), columns(q, C, 2 * C)
 
         planes[0] = fresh("planes0", [P, PACK, 2 * C], F32)
-        for j in range(PACK):
-            gather_plane(planes[0][:, j, 0:C], 0, j)
-            gather_plane(planes[0][:, j, C : 2 * C], 1, j)
+        gather_plane(planes[0][:, 0, 0:C], 0, 0, C)
+        gather_plane(planes[0][:, 0, C : 2 * C], 0, C, 2 * C)
+        for j in range(1, PACK):
+            gather_plane(planes[0][:, j, :], j, 0, 2 * C)
         for j in range(3):
             cast_plane(j)
-        both0 = weave_w("both0", w0[:], 0, K)
+        both = {0: weave_w("both0", w0[:], 0, K)}
         cast_plane(3)
-        quantize_w("lower0", both0[:, 0 : P * PACK], [0], 0)
-        gather(2)
+
+        def quantize_lower(e):
+            quantize_w("lower%d" % e, both[e][:, 0 : P * PACK], [e], 0)
+
+        quantize_lower(0)
+        gather(2, 4)
         weave_g(0, 2 * C)
-        g01 = quantize_fresh("g01", gb[0], 2 * C)
-        gq[0], gq[1] = columns(g01, 0, C), columns(g01, C, 2 * C)
-        gather(3, "gb0")
-        both1 = weave_w("both1", w1[:], 0, K)
-        weave_g(2, C)
-        quantize_w("lower1", both1[:, 0 : P * PACK], [1], 0)
-        quantize_g(2)
-        gather(4, "gb2")
-        lower23 = weave_w("lower23", w23[:], 0, P)
-        weave_g(3, C)
-        experts(0, [0, 1])
-        quantize_w("lower23", lower23, [2, 3], 0)
-        dyw = fresh("dyw", [P, T * PACK], BF16, "lower23")
+        quantize_pair(0)
+        gather(4, 5, "gb0")
+        for e, raw in ((1, w1), (2, w2), (3, w3)):
+            both[e] = weave_w("both%d" % e, raw[:], 0, K)
+            quantize_lower(e)
+        weave_g(2, 2 * C, "w2")
+        quantize_pair(2)
+        dyw = fresh("dyw", [P, T * PACK], BF16, "w2")
         nc.vector.tensor_copy(
             dyw[:].bitcast(F32).rearrange("p (c i u) -> p c u i", i=RUN, u=2),
             pairs[:].bitcast(F32).rearrange("p u (c i) -> p c u i", i=RUN),
         )
-        quantize_g(3)
-        gather(5, "gb3")
-        lower46 = weave_w("lower46", w465[:, 0:2], 0, P)
+        gather(5, 6, "pairs")
+        lower56 = weave_w("lower56", w56[:], 0, P)
         weave_g(4, C)
-        experts(0, [2, 3])
-        quantize_w("lower46", lower46, [4, 6], 0)
         quantize_g(4)
-        gather(6, "gb4")
-        lower5 = weave_w("lower5", w465[:, 2:3], 0, P)
-        weave_g(5, P)
-        upper23 = weave_w("upper23", w23[:], P, K)
+        gather(6, 7, "gb4")
+        experts(0, [0, 1])
+        both[4] = weave_w("both4", w4[:], 0, K)
+        experts(0, [2, 3])
+        weave_g(5, P, "w4")
         weave_g(6, P)
-        upper4 = weave_w("upper4", w465[:, 0:1], P, K)
-        experts(0, [4])
-        dyq = quantize_fresh("dy", dyw, T, "gate4")
-        quantize_w("lower5", lower5, [5], 0)
+        upper56 = weave_w("upper56", w56[:], P, K)
+        quantize_w("lower56", lower56, [5, 6], 0)
+        quantize_lower(4)
         quantize_g(5)
         quantize_g(6)
+        dyq = quantize_fresh("dy", dyw, T, "gb6")
+        experts(0, [4, 5, 6])
         ds0a = shared("ds0a", 0, dyq, 0, HALF)
-        experts(0, [5, 6])
         ds0b = shared("ds0b", 0, dyq, HALF, T)
-        upper65 = weave_w("upper65", w465[:, 1:3], P, K, "gb4", nc.vector.tensor_copy)
-        up = (fresh("up_codes", [P, (E + 1) * P], U32, "gb6")[:], fresh("up_scales", [P, (E + 1) * P], U8)[:])
-        quantize(*columns(up, 0, P), both0[:, P * PACK : K * PACK])
-        quantize(*columns(up, P, 2 * P), both1[:, P * PACK : K * PACK])
-        quantize(*columns(up, 2 * P, 4 * P), upper23[:])
-        quantize(*columns(up, 4 * P, 5 * P), upper4[:])
-        quantize(*columns(up, 5 * P, 7 * P), upper65[:])
-        for i, e in enumerate((0, 1, 2, 3, 4, 6, 5)):
-            wq[(e, 1)] = columns(up, i * P, (i + 1) * P)
+        up = (fresh("up_codes", [P, (E + 1) * P], U32, "w2")[:], fresh("up_scales", [P, (E + 1) * P], U8)[:])
+        for e in range(5):
+            quantize(*columns(up, e * P, (e + 1) * P), both[e][:, P * PACK : K * PACK])
+        quantize(*columns(up, 5 * P, 7 * P), upper56[:])
+        for e in range(E + 1):
+            wq[(e, 1)] = columns(up, e * P, (e + 1) * P)
         for cs in ([0, 1], [2, 3], [4, 5, 6]):
             experts(1, cs)
         ds1 = shared("ds1", 1, dyq, 0, T)

@@ -54,8 +54,8 @@ def tile_moe_bds_lin_none_kernel(tc, dyT, w, gate, offs, pos1, pos2, pos3, out):
         dy = [load_plane(0)]
         slots = load("slots", [P, S // 16], U16, offs)
         g01 = keep.tile([P, 2 * C], F32, name="gate01")
-        for e in range(2):
-            nc.sync.dma_start(g01[:, e * C : (e + 1) * C], gate[0:P, e * C : (e + 1) * C])
+        nc.scalar.dma_start(g01[:, 0:C], gate[0:P, 0:C])
+        nc.sync.dma_start(g01[:, C : 2 * C], gate[0:P, C : 2 * C])
         dy.extend(load_plane(j) for j in (1, 2))
         w0 = load_w("w0", [0])
         dy.append(load_plane(3))
@@ -64,8 +64,8 @@ def tile_moe_bds_lin_none_kernel(tc, dyT, w, gate, offs, pos1, pos2, pos3, out):
         w2 = load_w("w2", [2])
         w3 = load_w("w3", [3])
         g4 = load_gate(4, 6)
-        w56 = load_w("w56", [5, 6])
-        w4 = load_w("w4", [4])
+        w46 = load_w("w46", [4, 6])
+        w5 = load_w("w5", [5])
         back = [load("back%d" % r, [P, T // 16], U16, lst) for r, lst in enumerate((pos1, pos2, pos3))]
         gates = [g01, g2, g4]
         first = [0, C, 2 * C, 3 * C, 4 * C, 5 * C, 5 * C + P, S]
@@ -111,10 +111,10 @@ def tile_moe_bds_lin_none_kernel(tc, dyT, w, gate, offs, pos1, pos2, pos3, out):
             gb[c] = fresh("gb%d" % c, [P, width * PACK], BF16, tag)
             weave(nc.scalar.copy, gb[c][:], planes[c][:])
 
-        def weave_w(name, raw, k0, k1):
+        def weave_w(name, raw, k0, k1, tag=None, copy=nc.scalar.copy):
             n = raw.shape[1]
-            woven = fresh(name, [P, n * (k1 - k0) * PACK], BF16)
-            nc.scalar.copy(
+            woven = fresh(name, [P, n * (k1 - k0) * PACK], BF16, tag)
+            copy(
                 woven[:].rearrange("p (e c i t) -> p e c t i", e=n, i=RUN, t=PACK),
                 raw[:, :, :, k0:k1].rearrange("p e t (c i) -> p e c t i", i=RUN),
             )
@@ -138,11 +138,10 @@ def tile_moe_bds_lin_none_kernel(tc, dyT, w, gate, offs, pos1, pos2, pos3, out):
                 product(acc[:, first[c] - s0 : first[c + 1] - s0], wq[(first[c] // C, m)], gq[c])
             nc.scalar.copy(dx[m][:, s0:s1], acc[:, 0 : s1 - s0])
 
-        def shared(name, m, dyq, c0, c1):
-            acc = psum.tile([P, T], F32, name="acc")
-            product(acc[:, 0 : c1 - c0], wq[(E, m)], columns(dyq, c0, c1))
+        def shared(name, acc, m, dyq, c0, c1):
+            product(acc[:, c0:c1], wq[(E, m)], columns(dyq, c0, c1))
             tl = fresh(name, [P, c1 - c0], F32)
-            nc.scalar.copy(tl[:], acc[:, 0 : c1 - c0])
+            nc.scalar.copy(tl[:], acc[:, c0:c1])
             return tl
 
         def combine(m, part, rounds):
@@ -193,32 +192,32 @@ def tile_moe_bds_lin_none_kernel(tc, dyT, w, gate, offs, pos1, pos2, pos3, out):
             pairs[:].bitcast(F32).rearrange("p u (c i) -> p c u i", i=RUN),
         )
         gather(5, 6, "pairs")
-        lower56 = weave_w("lower56", w56[:], 0, P)
+        lower46 = weave_w("lower46", w46[:], 0, P)
         weave_g(4, C)
+        quantize_w("lower46", lower46, [4, 6], 0)
         quantize_g(4)
         gather(6, 7, "gb4")
         experts(0, [0, 1])
-        both[4] = weave_w("both4", w4[:], 0, K)
+        both[5] = weave_w("both5", w5[:], 0, K)
         experts(0, [2, 3])
-        weave_g(5, P, "w4")
+        weave_g(5, P, "w5")
         weave_g(6, P)
-        upper56 = weave_w("upper56", w56[:], P, K)
-        quantize_w("lower56", lower56, [5, 6], 0)
-        quantize_lower(4)
+        upper4 = weave_w("upper4", w46[:, 0:1], P, K)
+        dyq = quantize_fresh("dy", dyw, T, "gate4")
+        quantize_lower(5)
         quantize_g(5)
         quantize_g(6)
-        dyq = quantize_fresh("dy", dyw, T, "gb6")
+        acc0 = psum.tile([P, T], F32, name="acc")
+        ds0a = shared("ds0a", acc0, 0, dyq, 0, HALF)
         experts(0, [4, 5, 6])
-        ds0a = shared("ds0a", 0, dyq, 0, HALF)
-        ds0b = shared("ds0b", 0, dyq, HALF, T)
-        up = (fresh("up_codes", [P, (E + 1) * P], U32, "w2")[:], fresh("up_scales", [P, (E + 1) * P], U8)[:])
-        for e in range(5):
-            quantize(*columns(up, e * P, (e + 1) * P), both[e][:, P * PACK : K * PACK])
-        quantize(*columns(up, 5 * P, 7 * P), upper56[:])
+        ds0b = shared("ds0b", acc0, 0, dyq, HALF, T)
+        upper6 = weave_w("upper6", w46[:, 1:2], P, K, "gb4", nc.vector.tensor_copy)
+        uppers = [both[e][:, P * PACK : K * PACK] if e in both else (upper4, upper6)[e == E][:] for e in range(E + 1)]
+        up = (fresh("up_codes", [P, (E + 1) * P], U32, "gb6")[:], fresh("up_scales", [P, (E + 1) * P], U8)[:])
         for e in range(E + 1):
-            wq[(e, 1)] = columns(up, e * P, (e + 1) * P)
+            wq[(e, 1)] = quantize(*columns(up, e * P, (e + 1) * P), uppers[e])
         for cs in ([0, 1], [2, 3], [4, 5, 6]):
             experts(1, cs)
-        ds1 = shared("ds1", 1, dyq, 0, T)
+        ds1 = shared("ds1", psum.tile([P, T], F32, name="acc"), 1, dyq, 0, T)
         combine(0, [ds0a[:], ds0b[:]], [0, 1, 2])
         combine(1, [ds1[:, 0 : T - P], ds1[:, T - P : T]], [0, 1, 2])

@@ -6,12 +6,17 @@ K, T, E, C, N = 256, 512, 6, 256, 512
 S = E * C
 P = 128
 PACK = 4
+TOP = 3
+LIST_ROWS = 16
 RUN = 4
-HALF = T // 2
 SPARE = 16
 
+FIRST = (0, C, 2 * C, 3 * C, 4 * C, 5 * C, 5 * C + P, S)
+
+CUTS = ((0, T // 2, T), (0, T - P, T))
+
 FLOPS = 2 * N * K * (S + T)
-BYTES = 4 * (N * T + (E + 1) * N * K + S + K * T) + 2 * P * (S + 3 * T) // 16
+BYTES = 4 * (N * T + (E + 1) * N * K + S + K * T) + 2 * P * (S + TOP * T) // LIST_ROWS
 
 F32 = mybir.dt.float32
 BF16 = mybir.dt.bfloat16
@@ -29,195 +34,208 @@ def tile_moe_bds_lin_none_kernel(tc, dyT, w, gate, offs, pos1, pos2, pos3, out):
         keep = ctx.enter_context(tc.tile_pool(name="keep", bufs=1))
         psum = ctx.enter_context(tc.psum_pool(name="psum", bufs=8))
 
-        def load(name, shape, dtype, src):
-            tl = keep.tile(shape, dtype, name=name, tag=name, align_bytes=64)
-            nc.sync.dma_start(tl[:], src)
-            return tl
-
-        dy_rows = dyT.rearrange("(p j) c -> p j c", j=PACK)
-
-        def load_w(name, es):
-            tl = keep.tile([P, len(es), PACK, K], F32, name=name, tag=name, align_bytes=64)
-            for i, e in enumerate(es):
-                nc.sync.dma_start(tl[:, i], w[e].rearrange("(p j) k -> p j k", j=PACK))
-            return tl
-
-        def load_gate(c0, c1):
-            return load("gate%d" % c0, [P, (c1 - c0) * C], F32, gate[0:P, c0 * C : c1 * C])
-
-        def load_plane(j):
-            tl = keep.tile([P, T + SPARE], F32, name="dy%d" % j)
-            nc.gpsimd.memset(tl[:, T : T + SPARE], 0.0)
-            nc.sync.dma_start(tl[:, 0:T], dy_rows[:, j, :])
-            return tl
-
-        dy = [load_plane(0)]
-        slots = load("slots", [P, S // 16], U16, offs)
-        g01 = keep.tile([P, 2 * C], F32, name="gate01")
-        nc.scalar.dma_start(g01[:, 0:C], gate[0:P, 0:C])
-        nc.sync.dma_start(g01[:, C : 2 * C], gate[0:P, C : 2 * C])
-        dy.extend(load_plane(j) for j in (1, 2))
-        w0 = load_w("w0", [0])
-        dy.append(load_plane(3))
-        g2 = load_gate(2, 4)
-        w1 = load_w("w1", [1])
-        w2 = load_w("w2", [2])
-        w3 = load_w("w3", [3])
-        g4 = load_gate(4, 6)
-        w46 = load_w("w46", [4, 6])
-        w5 = load_w("w5", [5])
-        back = [load("back%d" % r, [P, T // 16], U16, lst) for r, lst in enumerate((pos1, pos2, pos3))]
-        gates = [g01, g2, g4]
-        first = [0, C, 2 * C, 3 * C, 4 * C, 5 * C, 5 * C + P, S]
-
-        def weave(copy, woven, planes):
-            copy(
-                woven.rearrange("p (c i t) -> p c t i", i=RUN, t=PACK),
-                planes.rearrange("p t (c i) -> p c t i", i=RUN),
-            )
-
         def fresh(name, shape, dtype, tag=None):
             return keep.tile(shape, dtype, name=name, tag=tag or name, align_bytes=64)
 
-        def quantize(codes, scales, woven):
-            nc.vector.quantize_mx(out=codes.bitcast(FP8X4), scales=scales, in_=woven)
-            return codes, scales
+        def load(name, shape, dtype, src):
+            dst = fresh(name, shape, dtype)
+            nc.sync.dma_start(dst[:], src)
+            return dst
 
-        def quantize_fresh(name, woven, width, tag=None):
-            codes = fresh(name + "_codes", [P, width], U32, tag)
-            scales = fresh(name + "_scales", [P, width], U8)
-            return quantize(codes[:], scales[:], woven[:, :])
+        def load_w(name, matrices):
+            dst = fresh(name, [P, len(matrices), PACK, K], F32)
+            for i, e in enumerate(matrices):
+                nc.sync.dma_start(dst[:, i], w[e].rearrange("(p t) k -> p t k", t=PACK))
+            return dst
 
-        def product(acc, wq, xq):
-            nc.tensor.matmul_mx(
-                out=acc, lhsT=wq[0].bitcast(FP8X4), lhsT_scale=wq[1],
-                rhs=xq[0].bitcast(FP8X4), rhs_scale=xq[1], start=True, stop=True,
-            )
+        def load_gate(e):
+            return load("gate%d" % e, [P, 2 * C], F32, gate[0:P, e * C : (e + 2) * C])
+
+        def load_plane(t):
+            dst = keep.tile([P, T + SPARE], F32, name="dy%d" % t)
+            nc.gpsimd.memset(dst[:, T : T + SPARE], 0.0)
+            nc.sync.dma_start(dst[:, 0:T], dyT.rearrange("(p t) c -> p t c", t=PACK)[:, t, :])
+            return dst
+
+        dy = [load_plane(0)]
+        slots = load("slots", [P, S // LIST_ROWS], U16, offs)
+        gate01 = keep.tile([P, 2 * C], F32, name="gate01")
+        nc.scalar.dma_start(gate01[:, 0:C], gate[0:P, 0:C])
+        nc.sync.dma_start(gate01[:, C : 2 * C], gate[0:P, C : 2 * C])
+        dy.extend(load_plane(t) for t in (1, 2))
+        w0 = load_w("w0", [0])
+        dy.append(load_plane(3))
+        gate23 = load_gate(2)
+        w1 = load_w("w1", [1])
+        w2 = load_w("w2", [2])
+        w3 = load_w("w3", [3])
+        gate45 = load_gate(4)
+        w46 = load_w("w46", [4, E])
+        w5 = load_w("w5", [5])
+        back = [load("back%d" % r, [P, T // LIST_ROWS], U16, pos) for r, pos in enumerate((pos1, pos2, pos3))]
+        gates = [gate01, gate23, gate45]
 
         dx = [keep.tile([P, S], F32, name="dx%d" % m) for m in range(2)]
-        cuts = [(0, HALF, T), (0, T - P, T)]
-        planes, gb, gq, wq, ds = {}, {}, {}, {}, {}
+        g_planes, g_woven = {}, {}
+        g_mx = {}
+        w_mx = {}
 
-        def gather_plane(dst, j, s0, s1):
-            g, o = divmod(s0, 2 * C)
-            nc.vector.tensor_tensor(dst, dy[j][:].indirect(slots[:, s0 // 16 : s1 // 16]), gates[g][:, o : o + s1 - s0], MULT)
+        def gather_plane(dst, t, s0, s1):
+            pair, offset = divmod(s0, 2 * C)
+            nc.vector.tensor_tensor(
+                dst,
+                dy[t][:].indirect(slots[:, s0 // LIST_ROWS : s1 // LIST_ROWS]),
+                gates[pair][:, offset : offset + s1 - s0],
+                MULT,
+            )
 
-        def gather(c, c1, tag=None):
-            planes[c] = fresh("planes%d" % c, [P, PACK, first[c1] - first[c]], F32, tag)
-            for j in range(PACK):
-                gather_plane(planes[c][:, j, :], j, first[c], first[c1])
+        def gather(c0, c1, tag=None):
+            g_planes[c0] = fresh("planes%d" % c0, [P, PACK, FIRST[c1] - FIRST[c0]], F32, tag)
+            for t in range(PACK):
+                gather_plane(g_planes[c0][:, t, :], t, FIRST[c0], FIRST[c1])
 
-        def weave_g(c, width, tag=None):
-            gb[c] = fresh("gb%d" % c, [P, width * PACK], BF16, tag)
-            weave(nc.scalar.copy, gb[c][:], planes[c][:])
+        def weave_g(c0, tag=None):
+            g_woven[c0] = fresh("gb%d" % c0, [P, g_planes[c0][:].shape[2] * PACK], BF16, tag)
+            nc.scalar.copy(
+                g_woven[c0][:].rearrange("p (c i t) -> p c t i", i=RUN, t=PACK),
+                g_planes[c0][:].rearrange("p t (c i) -> p c t i", i=RUN),
+            )
 
         def weave_w(name, raw, k0, k1, tag=None, copy=nc.scalar.copy):
-            n = raw.shape[1]
-            woven = fresh(name, [P, n * (k1 - k0) * PACK], BF16, tag)
+            count = raw.shape[1]
+            woven = fresh(name, [P, count * (k1 - k0) * PACK], BF16, tag)
             copy(
-                woven[:].rearrange("p (e c i t) -> p e c t i", e=n, i=RUN, t=PACK),
+                woven[:].rearrange("p (e c i t) -> p e c t i", e=count, i=RUN, t=PACK),
                 raw[:, :, :, k0:k1].rearrange("p e t (c i) -> p e c t i", i=RUN),
             )
             return woven
 
-        def columns(q, c0, c1):
-            return q[0][:, c0:c1], q[1][:, c0:c1]
+        def quantize(words, scales, woven):
+            nc.vector.quantize_mx(out=words.bitcast(FP8X4), scales=scales, in_=woven)
+            return words, scales
 
-        def quantize_g(c):
-            gq[c] = quantize_fresh("g%d" % c, gb[c], first[c + 1] - first[c])
+        def quantize_fresh(name, woven, width, tag=None):
+            words = fresh(name + "_codes", [P, width], U32, tag)
+            scales = fresh(name + "_scales", [P, width], U8)
+            return quantize(words[:], scales[:], woven)
 
-        def quantize_w(name, woven, es, m):
-            q = quantize_fresh(name, woven, len(es) * P)
-            for i, e in enumerate(es):
-                wq[(e, m)] = columns(q, i * P, (i + 1) * P)
+        def columns(operand, lo, hi):
+            return operand[0][:, lo:hi], operand[1][:, lo:hi]
 
-        def experts(m, cs):
+        def quantize_g(c0, c1):
+            s0 = FIRST[c0]
+            operand = quantize_fresh("g%d" % c0, g_woven[c0][:], FIRST[c1] - s0)
+            for c in range(c0, c1):
+                g_mx[c] = columns(operand, FIRST[c] - s0, FIRST[c + 1] - s0)
+
+        def quantize_lower(name, woven, matrices):
+            operand = quantize_fresh(name, woven, len(matrices) * P)
+            for i, e in enumerate(matrices):
+                w_mx[(e, 0)] = columns(operand, i * P, (i + 1) * P)
+
+        def product(acc, stationary, moving):
+            nc.tensor.matmul_mx(
+                out=acc,
+                lhsT=stationary[0].bitcast(FP8X4),
+                lhsT_scale=stationary[1],
+                rhs=moving[0].bitcast(FP8X4),
+                rhs_scale=moving[1],
+                start=True,
+                stop=True,
+            )
+
+        def experts(m, c0, c1):
             acc = psum.tile([P, T], F32, name="acc")
-            s0, s1 = first[cs[0]], first[cs[-1] + 1]
-            for c in cs:
-                product(acc[:, first[c] - s0 : first[c + 1] - s0], wq[(first[c] // C, m)], gq[c])
-            nc.scalar.copy(dx[m][:, s0:s1], acc[:, 0 : s1 - s0])
+            s0 = FIRST[c0]
+            for c in range(c0, c1):
+                product(acc[:, FIRST[c] - s0 : FIRST[c + 1] - s0], w_mx[(FIRST[c] // C, m)], g_mx[c])
+            nc.scalar.copy(dx[m][:, s0 : FIRST[c1]], acc[:])
 
-        def shared(name, acc, m, dyq, c0, c1):
-            product(acc[:, c0:c1], wq[(E, m)], columns(dyq, c0, c1))
-            tl = fresh(name, [P, c1 - c0], F32)
-            nc.scalar.copy(tl[:], acc[:, c0:c1])
-            return tl
+        def shared(name, acc, m, dy_mx, lo, hi):
+            product(acc[:, lo:hi], w_mx[(E, m)], columns(dy_mx, lo, hi))
+            ds = fresh(name, [P, hi - lo], F32)
+            nc.scalar.copy(ds[:], acc[:, lo:hi])
+            return ds
 
-        def combine(m, part, rounds):
-            for r in rounds:
+        def combine(m, sums):
+            for r in range(TOP):
                 for h in range(2):
-                    c0, c1 = cuts[m][h], cuts[m][h + 1]
-                    tl = fresh("sum%d_%d_%d" % (m, r, h), [P, c1 - c0], F32, None)
-                    nc.vector.tensor_tensor(tl[:], dx[m][:].indirect(back[r][:, c0 // 16 : c1 // 16]), part[h], ADD)
-                    part[h] = tl[:]
-                    if r == 2:
-                        nc.sync.dma_start(out[m * P : (m + 1) * P, c0:c1], tl[:])
+                    lo, hi = CUTS[m][h], CUTS[m][h + 1]
+                    total = fresh("sum%d_%d_%d" % (m, r, h), [P, hi - lo], F32)
+                    picked = dx[m][:].indirect(back[r][:, lo // LIST_ROWS : hi // LIST_ROWS])
+                    nc.vector.tensor_tensor(total[:], picked, sums[h], ADD)
+                    sums[h] = total[:]
+                    if r == TOP - 1:
+                        (nc.sync, nc.scalar)[h].dma_start(out[m * P : (m + 1) * P, lo:hi], total[:])
 
         pairs = fresh("pairs", [P, 2, 2 * T], BF16)
 
-        def cast_plane(j):
-            nc.scalar.copy(pairs[:, j // 2, j % 2 : 2 * T : 2], dy[j][:, 0:T])
+        def round_plane(t):
+            nc.scalar.copy(pairs[:, t // 2, t % 2 : 2 * T : 2], dy[t][:, 0:T])
 
-        def quantize_pair(c):
-            q = quantize_fresh("g%d" % c, gb[c], 2 * C)
-            gq[c], gq[c + 1] = columns(q, 0, C), columns(q, C, 2 * C)
+        whole = {}
 
-        planes[0] = fresh("planes0", [P, PACK, 2 * C], F32)
-        gather_plane(planes[0][:, 0, 0:C], 0, 0, C)
-        gather_plane(planes[0][:, 0, C : 2 * C], 0, C, 2 * C)
-        for j in range(1, PACK):
-            gather_plane(planes[0][:, j, :], j, 0, 2 * C)
-        for j in range(3):
-            cast_plane(j)
-        both = {0: weave_w("both0", w0[:], 0, K)}
-        cast_plane(3)
+        def lower_of_whole(e):
+            quantize_lower("lower%d" % e, whole[e][:, 0 : P * PACK], [e])
 
-        def quantize_lower(e):
-            quantize_w("lower%d" % e, both[e][:, 0 : P * PACK], [e], 0)
+        g_planes[0] = fresh("planes0", [P, PACK, 2 * C], F32)
+        gather_plane(g_planes[0][:, 0, 0:C], 0, 0, C)
+        gather_plane(g_planes[0][:, 0, C : 2 * C], 0, C, 2 * C)
+        for t in range(1, PACK):
+            gather_plane(g_planes[0][:, t, :], t, 0, 2 * C)
+        for t in range(PACK - 1):
+            round_plane(t)
+        whole[0] = weave_w("both0", w0[:], 0, K)
+        round_plane(PACK - 1)
+        lower_of_whole(0)
 
-        quantize_lower(0)
         gather(2, 4)
-        weave_g(0, 2 * C)
-        quantize_pair(0)
-        gather(4, 5, "gb0")
+        weave_g(0)
+        quantize_g(0, 2)
+        gather(4, 5, "planes0")
         for e, raw in ((1, w1), (2, w2), (3, w3)):
-            both[e] = weave_w("both%d" % e, raw[:], 0, K)
-            quantize_lower(e)
-        weave_g(2, 2 * C, "w2")
-        quantize_pair(2)
-        dyw = fresh("dyw", [P, T * PACK], BF16, "w2")
+            whole[e] = weave_w("both%d" % e, raw[:], 0, K)
+            lower_of_whole(e)
+        weave_g(2, "w2")
+        dy_woven = fresh("dyw", [P, T * PACK], BF16, "w3")
         nc.vector.tensor_copy(
-            dyw[:].bitcast(F32).rearrange("p (c i u) -> p c u i", i=RUN, u=2),
+            dy_woven[:].bitcast(F32).rearrange("p (c i u) -> p c u i", i=RUN, u=2),
             pairs[:].bitcast(F32).rearrange("p u (c i) -> p c u i", i=RUN),
         )
-        gather(5, 6, "pairs")
+        quantize_g(2, 4)
+
+        gather(5, 6, "planes2")
         lower46 = weave_w("lower46", w46[:], 0, P)
-        weave_g(4, C)
-        quantize_w("lower46", lower46, [4, 6], 0)
-        quantize_g(4)
-        gather(6, 7, "gb4")
-        experts(0, [0, 1])
-        both[5] = weave_w("both5", w5[:], 0, K)
-        experts(0, [2, 3])
-        weave_g(5, P, "w5")
-        weave_g(6, P)
+        weave_g(4)
+        quantize_lower("lower46", lower46[:], [4, E])
+        quantize_g(4, 5)
+        gather(6, 7, "planes0")
+        experts(0, 0, 2)
+        whole[5] = weave_w("both5", w5[:], 0, K)
+        experts(0, 2, 4)
+        weave_g(5, "w5")
+        weave_g(6)
         upper4 = weave_w("upper4", w46[:, 0:1], P, K)
-        dyq = quantize_fresh("dy", dyw, T, "gate4")
-        quantize_lower(5)
-        quantize_g(5)
-        quantize_g(6)
-        acc0 = psum.tile([P, T], F32, name="acc")
-        ds0a = shared("ds0a", acc0, 0, dyq, 0, HALF)
-        experts(0, [4, 5, 6])
-        ds0b = shared("ds0b", acc0, 0, dyq, HALF, T)
-        upper6 = weave_w("upper6", w46[:, 1:2], P, K, "gb4", nc.vector.tensor_copy)
-        uppers = [both[e][:, P * PACK : K * PACK] if e in both else (upper4, upper6)[e == E][:] for e in range(E + 1)]
-        up = (fresh("up_codes", [P, (E + 1) * P], U32, "gb6")[:], fresh("up_scales", [P, (E + 1) * P], U8)[:])
+
+        dy_mx = quantize_fresh("dy", dy_woven[:], T, "planes2")
+        lower_of_whole(5)
+        quantize_g(5, 6)
+        quantize_g(6, 7)
+        shared_acc = psum.tile([P, T], F32, name="acc")
+        ds_first = shared("ds0a", shared_acc, 0, dy_mx, 0, CUTS[0][1])
+        experts(0, 4, 7)
+        ds_second = shared("ds0b", shared_acc, 0, dy_mx, CUTS[0][1], T)
+
+        upper_shared = weave_w("upper6", w46[:, 1:2], P, K, "planes0", nc.vector.tensor_copy)
+        uppers = {e: whole[e][:, P * PACK : K * PACK] for e in whole}
+        uppers[4], uppers[E] = upper4[:], upper_shared[:]
+        upper_words = fresh("up_codes", [P, (E + 1) * P], U32, "gb6")
+        upper_scales = fresh("up_scales", [P, (E + 1) * P], U8)
         for e in range(E + 1):
-            wq[(e, 1)] = quantize(*columns(up, e * P, (e + 1) * P), uppers[e])
-        for cs in ([0, 1], [2, 3], [4, 5, 6]):
-            experts(1, cs)
-        ds1 = shared("ds1", psum.tile([P, T], F32, name="acc"), 1, dyq, 0, T)
-        combine(0, [ds0a[:], ds0b[:]], [0, 1, 2])
-        combine(1, [ds1[:, 0 : T - P], ds1[:, T - P : T]], [0, 1, 2])
+            w_mx[(e, 1)] = quantize(*columns((upper_words, upper_scales), e * P, (e + 1) * P), uppers[e])
+        for c0, c1 in ((0, 2), (2, 4), (4, 7)):
+            experts(1, c0, c1)
+        ds_upper = shared("ds1", psum.tile([P, T], F32, name="acc"), 1, dy_mx, 0, T)
+
+        combine(0, [ds_first[:], ds_second[:]])
+        combine(1, [ds_upper[:, 0 : CUTS[1][1]], ds_upper[:, CUTS[1][1] : T]])

from contextlib import ExitStack

import concourse.mybir as mybir

K, T, E, C, N = 256, 512, 6, 256, 512
S = E * C
P = 128
PACK = 4
TOP = 3
LIST_ROWS = 16
RUN = 4
SPARE = 16

FIRST = (0, C, 2 * C, 3 * C, 4 * C, 5 * C, 5 * C + P, S)

CUTS = ((0, T // 2, T), (0, T - P, T))

FLOPS = 2 * N * K * (S + T)
BYTES = 4 * (N * T + (E + 1) * N * K + S + K * T) + 2 * P * (S + TOP * T) // LIST_ROWS

F32 = mybir.dt.float32
BF16 = mybir.dt.bfloat16
U32 = mybir.dt.uint32
U16 = mybir.dt.uint16
U8 = mybir.dt.uint8
FP8X4 = mybir.dt.float8_e4m3fn_x4
MULT = mybir.AluOpType.mult
ADD = mybir.AluOpType.add


def tile_moe_bds_lin_none_kernel(tc, dyT, w, gate, offs, pos1, pos2, pos3, out):
    nc = tc.nc
    with ExitStack() as ctx:
        keep = ctx.enter_context(tc.tile_pool(name="keep", bufs=1))
        psum = ctx.enter_context(tc.psum_pool(name="psum", bufs=8))

        def fresh(name, shape, dtype, tag=None):
            return keep.tile(shape, dtype, name=name, tag=tag or name, align_bytes=64)

        def load(name, shape, dtype, src):
            dst = fresh(name, shape, dtype)
            nc.sync.dma_start(dst[:], src)
            return dst

        def load_w(name, matrices):
            dst = fresh(name, [P, len(matrices), PACK, K], F32)
            for i, e in enumerate(matrices):
                nc.sync.dma_start(dst[:, i], w[e].rearrange("(p t) k -> p t k", t=PACK))
            return dst

        def load_gate(e):
            return load("gate%d" % e, [P, 2 * C], F32, gate[0:P, e * C : (e + 2) * C])

        def load_plane(t):
            dst = keep.tile([P, T + SPARE], F32, name="dy%d" % t)
            nc.gpsimd.memset(dst[:, T : T + SPARE], 0.0)
            nc.sync.dma_start(dst[:, 0:T], dyT.rearrange("(p t) c -> p t c", t=PACK)[:, t, :])
            return dst

        dy = [load_plane(0)]
        slots = load("slots", [P, S // LIST_ROWS], U16, offs)
        gate01 = keep.tile([P, 2 * C], F32, name="gate01")
        nc.scalar.dma_start(gate01[:, 0:C], gate[0:P, 0:C])
        nc.sync.dma_start(gate01[:, C : 2 * C], gate[0:P, C : 2 * C])
        dy.extend(load_plane(t) for t in (1, 2))
        w0 = load_w("w0", [0])
        dy.append(load_plane(3))
        gate23 = load_gate(2)
        w1 = load_w("w1", [1])
        w2 = load_w("w2", [2])
        w3 = load_w("w3", [3])
        gate45 = load_gate(4)
        w46 = load_w("w46", [4, E])
        w5 = load_w("w5", [5])
        back = [load("back%d" % r, [P, T // LIST_ROWS], U16, pos) for r, pos in enumerate((pos1, pos2, pos3))]
        gates = [gate01, gate23, gate45]

        dx = [keep.tile([P, S], F32, name="dx%d" % m) for m in range(2)]
        g_planes, g_woven = {}, {}
        g_mx = {}
        w_mx = {}

        def gather_plane(dst, t, s0, s1):
            pair, offset = divmod(s0, 2 * C)
            nc.vector.tensor_tensor(
                dst,
                dy[t][:].indirect(slots[:, s0 // LIST_ROWS : s1 // LIST_ROWS]),
                gates[pair][:, offset : offset + s1 - s0],
                MULT,
            )

        def gather(c0, c1, tag=None):
            g_planes[c0] = fresh("planes%d" % c0, [P, PACK, FIRST[c1] - FIRST[c0]], F32, tag)
            for t in range(PACK):
                gather_plane(g_planes[c0][:, t, :], t, FIRST[c0], FIRST[c1])

        def weave_g(c0, tag=None):
            g_woven[c0] = fresh("gb%d" % c0, [P, g_planes[c0][:].shape[2] * PACK], BF16, tag)
            nc.scalar.copy(
                g_woven[c0][:].rearrange("p (c i t) -> p c t i", i=RUN, t=PACK),
                g_planes[c0][:].rearrange("p t (c i) -> p c t i", i=RUN),
            )

        def weave_w(name, raw, k0, k1, tag=None, copy=nc.scalar.copy):
            count = raw.shape[1]
            woven = fresh(name, [P, count * (k1 - k0) * PACK], BF16, tag)
            copy(
                woven[:].rearrange("p (e c i t) -> p e c t i", e=count, i=RUN, t=PACK),
                raw[:, :, :, k0:k1].rearrange("p e t (c i) -> p e c t i", i=RUN),
            )
            return woven

        def quantize(words, scales, woven):
            nc.vector.quantize_mx(out=words.bitcast(FP8X4), scales=scales, in_=woven)
            return words, scales

        def quantize_fresh(name, woven, width, tag=None):
            words = fresh(name + "_codes", [P, width], U32, tag)
            scales = fresh(name + "_scales", [P, width], U8)
            return quantize(words[:], scales[:], woven)

        def columns(operand, lo, hi):
            return operand[0][:, lo:hi], operand[1][:, lo:hi]

        def quantize_g(c0, c1):
            s0 = FIRST[c0]
            operand = quantize_fresh("g%d" % c0, g_woven[c0][:], FIRST[c1] - s0)
            for c in range(c0, c1):
                g_mx[c] = columns(operand, FIRST[c] - s0, FIRST[c + 1] - s0)

        def quantize_lower(name, woven, matrices):
            operand = quantize_fresh(name, woven, len(matrices) * P)
            for i, e in enumerate(matrices):
                w_mx[(e, 0)] = columns(operand, i * P, (i + 1) * P)

        def product(acc, stationary, moving):
            nc.tensor.matmul_mx(
                out=acc,
                lhsT=stationary[0].bitcast(FP8X4),
                lhsT_scale=stationary[1],
                rhs=moving[0].bitcast(FP8X4),
                rhs_scale=moving[1],
                start=True,
                stop=True,
            )

        def experts(m, c0, c1):
            acc = psum.tile([P, T], F32, name="acc")
            s0 = FIRST[c0]
            for c in range(c0, c1):
                product(acc[:, FIRST[c] - s0 : FIRST[c + 1] - s0], w_mx[(FIRST[c] // C, m)], g_mx[c])
            nc.scalar.copy(dx[m][:, s0 : FIRST[c1]], acc[:])

        def shared(name, acc, m, dy_mx, lo, hi):
            product(acc[:, lo:hi], w_mx[(E, m)], columns(dy_mx, lo, hi))
            ds = fresh(name, [P, hi - lo], F32)
            nc.scalar.copy(ds[:], acc[:, lo:hi])
            return ds

        def combine(m, sums):
            for r in range(TOP):
                for h in range(2):
                    lo, hi = CUTS[m][h], CUTS[m][h + 1]
                    total = fresh("sum%d_%d_%d" % (m, r, h), [P, hi - lo], F32)
                    picked = dx[m][:].indirect(back[r][:, lo // LIST_ROWS : hi // LIST_ROWS])
                    nc.vector.tensor_tensor(total[:], picked, sums[h], ADD)
                    sums[h] = total[:]
                    if r == TOP - 1:
                        (nc.sync, nc.scalar)[h].dma_start(out[m * P : (m + 1) * P, lo:hi], total[:])

        pairs = fresh("pairs", [P, 2, 2 * T], BF16)

        def round_plane(t):
            nc.scalar.copy(pairs[:, t // 2, t % 2 : 2 * T : 2], dy[t][:, 0:T])

        whole = {}

        def lower_of_whole(e):
            quantize_lower("lower%d" % e, whole[e][:, 0 : P * PACK], [e])

        g_planes[0] = fresh("planes0", [P, PACK, 2 * C], F32)
        gather_plane(g_planes[0][:, 0, 0:C], 0, 0, C)
        gather_plane(g_planes[0][:, 0, C : 2 * C], 0, C, 2 * C)
        for t in range(1, PACK):
            gather_plane(g_planes[0][:, t, :], t, 0, 2 * C)
        for t in range(PACK - 1):
            round_plane(t)
        whole[0] = weave_w("both0", w0[:], 0, K)
        round_plane(PACK - 1)
        lower_of_whole(0)

        gather(2, 4)
        weave_g(0)
        quantize_g(0, 2)
        gather(4, 5, "planes0")
        for e, raw in ((1, w1), (2, w2), (3, w3)):
            whole[e] = weave_w("both%d" % e, raw[:], 0, K)
            lower_of_whole(e)
        weave_g(2, "w2")
        dy_woven = fresh("dyw", [P, T * PACK], BF16, "w3")
        nc.vector.tensor_copy(
            dy_woven[:].bitcast(F32).rearrange("p (c i u) -> p c u i", i=RUN, u=2),
            pairs[:].bitcast(F32).rearrange("p u (c i) -> p c u i", i=RUN),
        )
        quantize_g(2, 4)

        gather(5, 6, "planes2")
        lower46 = weave_w("lower46", w46[:], 0, P)
        weave_g(4)
        quantize_lower("lower46", lower46[:], [4, E])
        quantize_g(4, 5)
        gather(6, 7, "planes0")
        experts(0, 0, 2)
        whole[5] = weave_w("both5", w5[:], 0, K)
        experts(0, 2, 4)
        weave_g(5, "w5")
        weave_g(6)
        upper4 = weave_w("upper4", w46[:, 0:1], P, K)

        dy_mx = quantize_fresh("dy", dy_woven[:], T, "planes2")
        lower_of_whole(5)
        quantize_g(5, 6)
        quantize_g(6, 7)
        shared_acc = psum.tile([P, T], F32, name="acc")
        ds_first = shared("ds0a", shared_acc, 0, dy_mx, 0, CUTS[0][1])
        experts(0, 4, 7)
        ds_second = shared("ds0b", shared_acc, 0, dy_mx, CUTS[0][1], T)

        upper_shared = weave_w("upper6", w46[:, 1:2], P, K, "planes0", nc.vector.tensor_copy)
        uppers = {e: whole[e][:, P * PACK : K * PACK] for e in whole}
        uppers[4], uppers[E] = upper4[:], upper_shared[:]
        upper_words = fresh("up_codes", [P, (E + 1) * P], U32, "gb6")
        upper_scales = fresh("up_scales", [P, (E + 1) * P], U8)
        for e in range(E + 1):
            w_mx[(e, 1)] = quantize(*columns((upper_words, upper_scales), e * P, (e + 1) * P), uppers[e])
        for c0, c1 in ((0, 2), (2, 4), (4, 7)):
            experts(1, c0, c1)
        ds_upper = shared("ds1", psum.tile([P, T], F32, name="acc"), 1, dy_mx, 0, T)

        combine(0, [ds_first[:], ds_second[:]])
        combine(1, [ds_upper[:, 0 : CUTS[1][1]], ds_upper[:, CUTS[1][1] : T]])
